import numpy as np
import ml_dtypes


def mxq(x, axis, fmt="e4m3"):
    dtype, down = {"e4m3": (ml_dtypes.float8_e4m3fn, 7), "e5m2": (ml_dtypes.float8_e5m2, 14)}[fmt]
    v = np.moveaxis(np.asarray(x, np.float32).astype(ml_dtypes.bfloat16).astype(np.float64), axis, -1)
    blocks = v.reshape(v.shape[:-1] + (-1, 32))
    amax = np.abs(blocks).max(-1, keepdims=True)
    byte = np.maximum(np.where(amax > 0, np.frexp(amax)[1] - 1 + 127, 0) - down, 1)
    scale = np.exp2(byte - 127.0)
    codes = (blocks / scale).astype(np.float32).astype(dtype).astype(np.float64)
    return np.moveaxis((codes * scale).reshape(v.shape), -1, axis)


WIDE = False


def mx_kscale(k):
    if not WIDE:
        return np.ones(k)
    levels = np.array([10, -10, 5, -5, 0])
    if k % 512:
        return np.exp2(np.random.permutation(np.resize(levels, k // 32))).repeat(32)
    a = np.empty((k // 512, 16))
    for p in range(k // 512):
        a[p, :8] = np.random.permutation(np.resize(levels, 8))
        for g in range(8):
            far = levels[np.abs(levels - a[p, g]) >= 10]
            a[p, g + 8] = far[np.random.randint(len(far))]
    return np.exp2(a.ravel()).repeat(32)


def f64(x):
    return np.asarray(x).astype(np.float64)


def striped(idx):
    return np.tile(np.asarray(idx).reshape(-1, 16).T, (8, 1)).astype(np.uint16)


def unstriped(offs):
    return offs[:16].T.reshape(-1).astype(np.int64)


E2M1 = np.array([0.0, 0.5, 1.0, 1.5, 2.0, 3.0, 4.0, 6.0, -0.0, -0.5, -1.0, -1.5, -2.0, -3.0, -4.0, -6.0])


def pack_weight(w, fmt):
    k, n = w.shape
    w = f64(np.asarray(w, np.float32).astype(ml_dtypes.bfloat16)).reshape(k // 32, 32, n)
    amax = np.abs(w).max(1)
    if fmt == "e4m3":
        byte = np.frexp(amax)[1] - 1 + 127 - 7
    else:
        mant, ex = np.frexp(amax / 6.0)
        byte = np.where(mant > 0.5, ex, ex - 1) + 127
    byte = np.clip(np.where(amax > 0, byte, 1), 1, 254)
    scaled = (w * np.exp2(127.0 - byte)[:, None, :]).reshape(k, n).astype(np.float32)
    by_word = np.ascontiguousarray(scaled.reshape(k // 512, 128, 4, n).transpose(0, 1, 3, 2))
    if fmt == "e4m3":
        words = by_word.astype(ml_dtypes.float8_e4m3fn).view(np.uint8)
    else:
        c = by_word.astype(ml_dtypes.float4_e2m1fn).view(np.uint8) & 0xF
        words = (c[..., 0::2] | (c[..., 1::2] << 4)).reshape(k // 512, 128, 2 * n)
    return np.ascontiguousarray(words), np.ascontiguousarray(byte.astype(np.uint8).reshape(k // 512, 16, n))


def unpack_weight(words, scales, fmt):
    g, _, n = scales.shape
    words = np.ascontiguousarray(words).reshape(g, 128, n, -1)
    if fmt == "e4m3":
        vals = words.view(ml_dtypes.float8_e4m3fn).astype(np.float64)
    else:
        nib = np.empty((g, 128, n, 4), np.uint8)
        nib[..., 0::2] = words & 0xF
        nib[..., 1::2] = words >> 4
        vals = E2M1[nib]
    vals = vals * np.repeat(np.exp2(scales.astype(np.float64) - 127.0), 8, axis=1)[..., None]
    return vals.transpose(0, 1, 3, 2).reshape(g * 512, n)


def bf(x):
    return np.asarray(x, np.float32).astype(ml_dtypes.bfloat16)


def planes(Y):
    r, m = Y.shape
    b = f64(bf(Y)).reshape(r // 32, 32, m)
    amax = np.abs(b).max(1)
    byte = np.clip(np.where(amax > 0, np.frexp(amax)[1] - 1 + 127 - 7, 1), 1, 254)
    codes = (b * np.exp2(127.0 - byte)[:, None, :]).reshape(r, m).astype(np.float32).astype(ml_dtypes.float8_e4m3fn).view(np.uint8)
    words = codes.reshape(r // 512, 128, 4, m).transpose(0, 1, 3, 2)
    return np.ascontiguousarray(words), np.ascontiguousarray(byte.astype(np.uint8).reshape(r // 512, 16, m))


C, I, J, T, R, N = 2048, 512, 512, 512, 512, 512


def setup_inputs():
    n = np.random.standard_normal
    idx = np.random.permutation(C)[:I]
    idx2 = np.random.permutation(C)[:J]
    fi = mx_kscale(I)
    fj = mx_kscale(J)
    fr = mx_kscale(R)
    wap = pack_weight(n((I, R)) * 1 / np.sqrt(I) * fi[:, None] * fr, "e2m1")
    vap = pack_weight(n((R, N)) * 1 / np.sqrt(R) / fr[:, None], "e4m3")
    wbp = pack_weight(n((J, N)) * 1 / np.sqrt(J) * fj[:, None], "e2m1")
    return {
        "xt": (n((T, C))).astype(np.float32),
        "fi": (np.random.uniform(0.5, 2.0, (I, 1)) / fi[:, None]).astype(np.float32),
        "fj": (np.random.uniform(0.5, 2.0, (J, 1)) / fj[:, None]).astype(np.float32),
        "wa_words": wap[0],
        "wa_scales": wap[1],
        "va_words": vap[0],
        "va_scales": vap[1],
        "wb_words": wbp[0],
        "wb_scales": wbp[1],
        "offs": striped(idx),
        "offs2": striped(idx2),
    }


def reference(xt, fi, fj, wa_words, wa_scales, va_words, va_scales, wb_words, wb_scales, offs, offs2):
    idx = unstriped(offs)
    idx2 = unstriped(offs2)
    wau = unpack_weight(wa_words, wa_scales, "e2m1")
    vau = unpack_weight(va_words, va_scales, "e4m3")
    wbu = unpack_weight(wb_words, wb_scales, "e2m1")
    xi = f64(xt)[:, idx].T
    xa = xi * f64(fi)
    xj = f64(xt)[:, idx2].T
    xb = xj * f64(fj)
    xaq = mxq(xa, 0, "e4m3")
    a = wau.T @ xaq
    hid = np.maximum(a, 0.0)
    hidq = mxq(hid, 0, "e4m3")
    xbq = mxq(xb, 0, "e4m3")
    y = vau.T @ hidq + wbu.T @ xbq
    words, scales = planes(y)
    return y, words, scales

@@ -1,0 +1,205 @@
+from contextlib import ExitStack
+
+import concourse.mybir as mybir
+from concourse.masks import make_identity
+
+C, K, T = 2048, 512, 512
+P = 128
+PACK = 4
+TILES = T // P
+ROOM = 4 * C
+FLOPS = 3 * 2 * K * K * T
+
+F32 = mybir.dt.float32
+BF16 = mybir.dt.bfloat16
+I32 = mybir.dt.int32
+U32 = mybir.dt.uint32
+U16 = mybir.dt.uint16
+U8 = mybir.dt.uint8
+FP8X4 = mybir.dt.float8_e4m3fn_x4
+FP4X4 = mybir.dt.float4_e2m1fn_x4
+MULT = mybir.AluOpType.mult
+COPY = mybir.ActivationFunctionType.Copy
+RELU = mybir.ActivationFunctionType.Relu
+
+
+def tile_list_feature_experts_pl_kernel(
+    tc, xt, fi, fj, wa_words, wa_scales, va_words, va_scales, wb_words, wb_scales, offs, offs2, out_0, out_1, out_2
+):
+    nc = tc.nc
+    with ExitStack() as ctx:
+        lists = ctx.enter_context(tc.tile_pool(name="lists", bufs=1))
+        keep = ctx.enter_context(tc.tile_pool(name="keep", bufs=1))
+        shared = ctx.enter_context(tc.tile_pool(name="shared", bufs=1))
+        turn_ps = ctx.enter_context(tc.psum_pool(name="turn_ps", bufs=3))
+        hid_ps = ctx.enter_context(tc.psum_pool(name="hid_ps", bufs=2))
+        out_ps = ctx.enter_context(tc.psum_pool(name="out_ps", bufs=3))
+
+        list_a = lists.tile([P, K // 16], U16, name="list_a")
+        list_b = lists.tile([P, K // 16], U16, name="list_b")
+        factor_a = keep.tile([P, PACK], F32, name="factor_a")
+        factor_b = keep.tile([P, PACK], F32, name="factor_b")
+        rooms = {}
+        top = [0]
+        pins = {"yb0":"gb3","yb1":"gb3","yb2":"gb3","qh1":"gb3","qh2":"gb3","qb2":"gb3","qa2":"gb3","qh0":"gb2","dwb":"gb2","dva":"gb2","d2":"gb2","yf0":"cb3","d1":"gb0"}
+
+        def place(shape, dtype, size, name, room):
+            if name in pins:
+                base, fill = rooms[pins[name]]
+                start = base + fill
+                rooms[pins[name]] = (base, fill + size)
+            else:
+                start = top[0]
+                top[0] = top[0] + size
+            if room:
+                rooms[room] = (start, 0)
+            return shared.tile(shape, dtype, name=name, offset=start, align_bytes=64)
+
+        tokens = [place([P, C], F32, 4 * C, "x%d" % k, "gb%d" % k) for k in range(TILES)]
+        wa_raw = keep.tile([P, K], U16, name="wa_raw")
+        wb_raw = keep.tile([P, K], U16, name="wb_raw")
+        va_raw = keep.tile([P, K], I32, name="va_raw")
+        scales_raw = keep.tile([P, 2 * K], U8, name="scales_raw")
+        first_raw, second_raw = scales_raw[:, 0:K], scales_raw[:, K : 2 * K]
+        ident = keep.tile([P, P], F32, name="ident")
+
+        nc.gpsimd.memset(scales_raw[:].bitcast(U32), 0)
+        make_identity(nc, ident[:])
+
+        t = {}
+        out_scales = keep.tile([P, T], U8, name="out_scales", align_bytes=64)
+        out_rows = out_0.rearrange("(p j) t -> p j t", j=PACK)
+        out_words = out_1[0].rearrange("p t r -> p (t r)").bitcast(I32)
+        queues = {"sp": nc.sync, "act": nc.scalar}
+        planes = {"wa": (first_raw, 0, wa_scales), "wb": (second_raw, 0, wb_scales), "va": (second_raw, 4, va_scales)}
+
+        def load(queue, name):
+            if name == "o1":
+                queue.dma_start(list_a[:], offs)
+            elif name == "o2":
+                queue.dma_start(list_b[:], offs2)
+            elif name == "fi":
+                queue.dma_start(out=factor_a[:], in_=fi.rearrange("(p j) o -> p (j o)", j=PACK))
+            elif name == "fj":
+                queue.dma_start(out=factor_b[:], in_=fj.rearrange("(p j) o -> p (j o)", j=PACK))
+            elif name[0] == "x":
+                k = int(name[1])
+                queue.dma_start(out=tokens[k][:], in_=xt[k * P : (k + 1) * P, :])
+            elif name == "wa":
+                queue.dma_start(out=wa_raw[:].bitcast(I32), in_=wa_words[0].bitcast(I32))
+            elif name == "wb":
+                queue.dma_start(out=wb_raw[:].bitcast(I32), in_=wb_words[0].bitcast(I32))
+            elif name == "va":
+                queue.dma_start(out=va_raw[:], in_=va_words[0].rearrange("p n t -> p (n t)").bitcast(I32))
+            else:
+                plane, row, scales = planes[name[1:3]]
+                q = int(name[3])
+                queue.dma_start(
+                    out=plane[32 * q + row : 32 * q + row + 4, :].bitcast(I32),
+                    in_=scales[0, 4 * q : 4 * q + 4, :].bitcast(I32),
+                )
+
+        def step(name):
+            kind, key = name[0], name[1:]
+            if name[0:2] == "L:":
+                parts = name.split(":")
+                load(queues[parts[1]], parts[2])
+            elif name[0:3] == "row":
+                factor = factor_a if name == "rowa" else factor_b
+                bank = turn_ps.tile([P, PACK, P], F32, tag="turn", name=name + "_bank")
+                for j in range(PACK):
+                    nc.tensor.transpose(bank[:, j, :], factor[:, j : j + 1].to_broadcast([P, P]), ident[:])
+                t[name] = place([P, K], F32, 4 * K, name, "g" + name[3] + "last")
+                dst, src = t[name][:].rearrange("q (n j) -> q n j", j=PACK), bank[:].rearrange("q j n -> q n j")
+                if name == "rowb":
+                    nc.scalar.activation(out=dst, in_=src, func=COPY)
+                else:
+                    nc.vector.tensor_copy(out=dst, in_=src)
+            elif kind == "d":
+                raw, dtype, size = {"wa": (wa_raw, U16, 2), "wb": (wb_raw, U16, 2), "va": (va_raw, I32, 4), "1": (first_raw, U8, 1), "2": (second_raw, U8, 1)}[key]
+                t[name] = place([P, K], dtype, size * K, name, None)
+                nc.vector.tensor_copy(
+                    out=t[name][:].rearrange("p (j q) -> p j q", j=PACK), in_=raw[:].rearrange("p (q j) -> p j q", j=PACK)
+                )
+            elif kind == "g":
+                t[name] = place([P, K], F32, 4 * K, name, "c" + key)
+                offsets = list_a if key[0] == "a" else list_b
+                nc.vector.tensor_tensor(t[name][:], tokens[int(key[1])][:].indirect(offsets[:]), t["row" + key[0]][:], MULT)
+            elif kind == "c":
+                t[name] = place([P, K], BF16, 2 * K, name, "T" + key)
+                nc.scalar.copy(
+                    out=t[name][:].rearrange("t (u p e) -> t u p e", u=2, e=2),
+                    in_=t["g" + key][:].rearrange("t (p u e) -> t u p e", u=2, e=2),
+                )
+            elif kind == "T":
+                words = t["c" + key][:].bitcast(F32)
+                t[name] = turn_ps.tile([P, PACK, P], F32, tag="turn", name=name)
+                for u in range(2):
+                    nc.tensor.transpose(t[name][:, u, :], words[:, u * P : (u + 1) * P], ident[:])
+            elif kind == "e":
+                t[name] = place([P, K], BF16, 2 * K, name, "q" + key)
+                nc.scalar.copy(
+                    out=t[name][:].bitcast(F32).rearrange("p (t u) -> p t u", u=2),
+                    in_=t["T" + key][:, 0:2, :].rearrange("p u t -> p t u"),
+                )
+            elif kind == "q":
+                k = int(key[1])
+                src = t[{"a": "ea", "b": "eb", "h": "r", "y": "yb"}[key[0]] + key[1]]
+                codes = place([P, P], U32, 4 * P, name, None)
+                if key[0] == "y":
+                    cols = slice(k * P, (k + 1) * P)
+                    nc.vector.quantize_mx(out=codes[:].bitcast(FP8X4), scales=out_scales[:, cols], in_=src[:])
+                    nc.sync.dma_start(out=out_words[:, cols], in_=codes[:].bitcast(I32))
+                else:
+                    scales = keep.tile([P, P], U8, name=name + "_scales", align_bytes=64)
+                    nc.vector.quantize_mx(out=codes[:].bitcast(FP8X4), scales=scales[:], in_=src[:])
+                    t[name] = (codes, scales)
+            elif kind == "m":
+                k = key[1]
+                weight, dtype, plane, row, operand = {
+                    "1": ("dwa", FP4X4, "d1", 0, "qa"), "b": ("dwb", FP4X4, "d2", 0, "qb"), "v": ("dva", FP8X4, "d2", 4, "qh"),
+                }[key[0]]
+                codes, scales = t[operand + k]
+                if key[0] == "1":
+                    bank = hid_ps.tile([P, PACK, P], F32, tag="hid", name=name)
+                    t["hid" + k] = bank
+                    first, last = True, True
+                elif "out" + k in t:
+                    bank = t["out" + k]
+                    first, last = False, True
+                else:
+                    bank = out_ps.tile([P, PACK, P], F32, tag="out", name=name)
+                    t["out" + k] = bank
+                    first, last = True, False
+                for j in range(PACK):
+                    cols = slice(j * P, (j + 1) * P)
+                    alone = key[0] == "1"
+                    nc.tensor.matmul_mx(
+                        out=bank[:, j, :], lhsT=t[weight][:, cols].bitcast(dtype), lhsT_scale=t[plane][row:P, cols],
+                        rhs=codes[:].bitcast(FP8X4), rhs_scale=scales[:],
+                        start=first and (alone or j == 0), stop=last and (alone or j == PACK - 1),
+                    )
+            elif kind == "r":
+                t[name] = place([P, K], BF16, 2 * K, name, "qh" + key)
+                nc.scalar.activation(
+                    out=t[name][:].rearrange("p (t j) -> p t j", j=PACK), in_=t["hid" + key][:].rearrange("p j t -> p t j"), func=RELU
+                )
+            elif name[0:2] == "yf":
+                k = int(name[2])
+                t[name] = place([P, PACK, P], F32, 4 * K, name, None)
+                nc.scalar.copy(out=t[name][:], in_=t["out" + name[2]][:])
+                nc.sync.dma_start(out=out_rows[:, :, k * P : (k + 1) * P], in_=t[name][:])
+            elif name[0:2] == "yb":
+                t[name] = place([P, K], BF16, 2 * K, name, "qy" + name[2])
+                nc.vector.tensor_copy(
+                    out=t[name][:].rearrange("p (t j) -> p t j", j=PACK), in_=t["yf" + name[2]][:].rearrange("p j t -> p t j")
+                )
+
+        for name in "L:sp:o1 L:act:fi L:sp:o2 L:act:fj L:sp:wa L:act:swa0 L:sp:x0 L:act:swa1 L:act:swa2 L:act:swa3 rowa rowb L:act:sva0 L:act:sva1 L:act:sva2 L:act:sva3 L:sp:x1 L:sp:x2 L:sp:wb L:sp:va L:sp:swb0 L:sp:swb1 L:sp:swb2 L:sp:swb3 L:sp:x3 dwa ga0 ca0 Ta0 ea0 gb0 cb0 Tb0 eb0 d1 ga1 ca1 Ta1 ea1 qa0 m10 r0 gb1 cb1 Tb1 eb1 ga2 ca2 Ta2 ea2 qa1 m11 r1 gb2 cb2 Tb2 eb2 dwb dva d2 qb0 mb0 qh0 mv0 qb1 mb1 ga3 ca3 Ta3 ea3 gb3 cb3 Tb3 eb3 qa2 m12 r2 qa3 m13 r3 yf0 qh1 mv1 yf1 qb2 mb2 qb3 mb3 qh2 mv2 yf2 qh3 mv3 yf3 yb0 qy0 yb1 qy1 yb2 qy2 yb3 qy3".split():
+            step(name)
+
+        for q in range(4):
+            queue = nc.sync if q < 2 else nc.scalar
+            queue.dma_start(
+                out=out_2[0, 4 * q : 4 * q + 4, :].bitcast(I32), in_=out_scales[32 * q : 32 * q + 4, :].bitcast(I32)
+            )

@@ -37,11 +37,9 @@ def tile_list_feature_experts_pl_kernel(
 
         list_a = lists.tile([P, K // 16], U16, name="list_a")
         list_b = lists.tile([P, K // 16], U16, name="list_b")
-        factor_a = keep.tile([P, PACK], F32, name="factor_a")
-        factor_b = keep.tile([P, PACK], F32, name="factor_b")
         rooms = {}
         top = [0]
-        pins = {"yb0":"gb3","yb1":"gb3","yb2":"gb3","qh1":"gb3","qh2":"gb3","qb2":"gb3","qa2":"gb3","qh0":"gb2","dwb":"gb2","dva":"gb2","d2":"gb2","yf0":"cb3","d1":"gb0"}
+        pins = {"ga0":"factors","ga2":"qa0","ga3":"qa1","gb2":"galast","gb3":"qa3","dwb":"gb2","dva":"gb2","d2":"gb2","qh2":"gb3","qh3":"gb3","qb2":"gb3","yb0":"gb3","yb1":"gb3","ca1":"Ta0","cb1":"Tb0","ca2":"Ta1","ca3":"Tb1","cb2":"Ta2","ga1":"factors","d1":"ca1","dwa":"ca1"}
 
         def place(shape, dtype, size, name, room):
             if name in pins:
@@ -56,10 +54,15 @@ def tile_list_feature_experts_pl_kernel(
             return shared.tile(shape, dtype, name=name, offset=start, align_bytes=64)
 
         tokens = [place([P, C], F32, 4 * C, "x%d" % k, "gb%d" % k) for k in range(TILES)]
+        first_picks = top[0]
+        top[0] = top[0] + 8 * K
+        factors = shared.tile([P, 16], F32, name="factors", offset=first_picks + 4 * K - 32)
+        factor_a, factor_b = factors[:, 0:PACK], factors[:, 8 : 8 + PACK]
+        rooms["factors"] = (first_picks, 0)
         wa_raw = keep.tile([P, K], U16, name="wa_raw")
         wb_raw = keep.tile([P, K], U16, name="wb_raw")
         va_raw = keep.tile([P, K], I32, name="va_raw")
-        scales_raw = keep.tile([P, 2 * K], U8, name="scales_raw")
+        scales_raw = place([P, 2 * K], U8, 4 * K, "scales_raw", "d2")
         first_raw, second_raw = scales_raw[:, 0:K], scales_raw[:, K : 2 * K]
         ident = keep.tile([P, P], F32, name="ident")
 
@@ -109,12 +112,9 @@ def tile_list_feature_experts_pl_kernel(
                 bank = turn_ps.tile([P, PACK, P], F32, tag="turn", name=name + "_bank")
                 for j in range(PACK):
                     nc.tensor.transpose(bank[:, j, :], factor[:, j : j + 1].to_broadcast([P, P]), ident[:])
-                t[name] = place([P, K], F32, 4 * K, name, "g" + name[3] + "last")
+                t[name] = place([P, K], F32, 8 * K, name, "g" + name[3] + "last")
                 dst, src = t[name][:].rearrange("q (n j) -> q n j", j=PACK), bank[:].rearrange("q j n -> q n j")
-                if name == "rowb":
-                    nc.scalar.activation(out=dst, in_=src, func=COPY)
-                else:
-                    nc.vector.tensor_copy(out=dst, in_=src)
+                nc.vector.tensor_copy(out=dst, in_=src)
             elif kind == "d":
                 raw, dtype, size = {"wa": (wa_raw, U16, 2), "wb": (wb_raw, U16, 2), "va": (va_raw, I32, 4), "1": (first_raw, U8, 1), "2": (second_raw, U8, 1)}[key]
                 t[name] = place([P, K], dtype, size * K, name, None)
@@ -127,17 +127,19 @@ def tile_list_feature_experts_pl_kernel(
                 nc.vector.tensor_tensor(t[name][:], tokens[int(key[1])][:].indirect(offsets[:]), t["row" + key[0]][:], MULT)
             elif kind == "c":
                 t[name] = place([P, K], BF16, 2 * K, name, "T" + key)
-                nc.scalar.copy(
-                    out=t[name][:].rearrange("t (u p e) -> t u p e", u=2, e=2),
-                    in_=t["g" + key][:].rearrange("t (p u e) -> t u p e", u=2, e=2),
-                )
+                dst = t[name][:].rearrange("t (u p e) -> t u p e", u=2, e=2)
+                src = t["g" + key][:].rearrange("t (p u e) -> t u p e", u=2, e=2)
+                if name in ["cb3"]:
+                    nc.vector.tensor_copy(out=dst, in_=src)
+                else:
+                    nc.scalar.activation(out=dst, in_=src, func=COPY)
             elif kind == "T":
                 words = t["c" + key][:].bitcast(F32)
                 t[name] = turn_ps.tile([P, PACK, P], F32, tag="turn", name=name)
                 for u in range(2):
                     nc.tensor.transpose(t[name][:, u, :], words[:, u * P : (u + 1) * P], ident[:])
             elif kind == "e":
-                t[name] = place([P, K], BF16, 2 * K, name, "q" + key)
+                t[name] = place([P, K], BF16, 4 * K, name, "q" + key)
                 nc.scalar.copy(
                     out=t[name][:].bitcast(F32).rearrange("p (t u) -> p t u", u=2),
                     in_=t["T" + key][:, 0:2, :].rearrange("p u t -> p t u"),
@@ -195,7 +197,7 @@ def tile_list_feature_experts_pl_kernel(
                     out=t[name][:].rearrange("p (t j) -> p t j", j=PACK), in_=t["yf" + name[2]][:].rearrange("p j t -> p t j")
                 )
 
-        for name in "L:sp:o1 L:act:fi L:sp:o2 L:act:fj L:sp:wa L:act:swa0 L:sp:x0 L:act:swa1 L:act:swa2 L:act:swa3 rowa rowb L:act:sva0 L:act:sva1 L:act:sva2 L:act:sva3 L:sp:x1 L:sp:x2 L:sp:wb L:sp:va L:sp:swb0 L:sp:swb1 L:sp:swb2 L:sp:swb3 L:sp:x3 dwa ga0 ca0 Ta0 ea0 gb0 cb0 Tb0 eb0 d1 ga1 ca1 Ta1 ea1 qa0 m10 r0 gb1 cb1 Tb1 eb1 ga2 ca2 Ta2 ea2 qa1 m11 r1 gb2 cb2 Tb2 eb2 dwb dva d2 qb0 mb0 qh0 mv0 qb1 mb1 ga3 ca3 Ta3 ea3 gb3 cb3 Tb3 eb3 qa2 m12 r2 qa3 m13 r3 yf0 qh1 mv1 yf1 qb2 mb2 qb3 mb3 qh2 mv2 yf2 qh3 mv3 yf3 yb0 qy0 yb1 qy1 yb2 qy2 yb3 qy3".split():
+        for name in "L:sp:o1 L:act:fi L:sp:o2 L:act:fj L:sp:x0 L:act:swa0 L:act:swa1 L:act:swa2 L:act:swa3 rowa rowb L:sp:wa L:sp:x1 L:sp:x2 L:sp:wb L:sp:va L:sp:x3 L:sp:swb0 L:sp:swb1 L:sp:swb2 L:sp:swb3 L:sp:sva0 L:sp:sva1 L:sp:sva2 L:sp:sva3 ga0 ca0 Ta0 gb0 cb0 Tb0 ea0 ga1 ca1 Ta1 eb0 gb1 cb1 Tb1 ea1 d1 dwa qa0 m10 qb0 ga2 ca2 Ta2 eb1 r0 qa1 m11 ga3 ca3 Ta3 ea2 r1 qb1 gb2 cb2 Tb2 ea3 qa2 m12 dwb dva qh0 qh1 d2 qa3 m13 mb0 mv0 mb1 mv1 eb2 r2 r3 yf0 yf1 gb3 cb3 Tb3 eb3 qh2 qb2 qh3 qb3 mb2 mv2 mv3 mb3 yf2 yf3 yb0 qy0 yb1 qy1 yb2 qy2 yb3 qy3".split():
             step(name)
 
         for q in range(4):

from contextlib import ExitStack

import concourse.mybir as mybir
from concourse.masks import make_identity

C, K, T = 2048, 512, 512
P = 128
PACK = 4
TILES = T // P
ROOM = 4 * C
FLOPS = 3 * 2 * K * K * T

F32 = mybir.dt.float32
BF16 = mybir.dt.bfloat16
I32 = mybir.dt.int32
U32 = mybir.dt.uint32
U16 = mybir.dt.uint16
U8 = mybir.dt.uint8
FP8X4 = mybir.dt.float8_e4m3fn_x4
FP4X4 = mybir.dt.float4_e2m1fn_x4
MULT = mybir.AluOpType.mult
COPY = mybir.ActivationFunctionType.Copy
RELU = mybir.ActivationFunctionType.Relu


def tile_list_feature_experts_pl_kernel(
    tc, xt, fi, fj, wa_words, wa_scales, va_words, va_scales, wb_words, wb_scales, offs, offs2, out_0, out_1, out_2
):
    nc = tc.nc
    with ExitStack() as ctx:
        lists = ctx.enter_context(tc.tile_pool(name="lists", bufs=1))
        keep = ctx.enter_context(tc.tile_pool(name="keep", bufs=1))
        shared = ctx.enter_context(tc.tile_pool(name="shared", bufs=1))
        turn_ps = ctx.enter_context(tc.psum_pool(name="turn_ps", bufs=3))
        hid_ps = ctx.enter_context(tc.psum_pool(name="hid_ps", bufs=2))
        out_ps = ctx.enter_context(tc.psum_pool(name="out_ps", bufs=3))

        list_a = lists.tile([P, K // 16], U16, name="list_a")
        list_b = lists.tile([P, K // 16], U16, name="list_b")
        rooms = {}
        top = [0]
        pins = {"ga0":"factors","ga2":"qa0","ga3":"qa1","gb2":"galast","gb3":"qa3","dwb":"gb2","dva":"gb2","d2":"gb2","qh2":"gb3","qh3":"gb3","qb2":"gb3","yb0":"gb3","yb1":"gb3","ca1":"Ta0","cb1":"Tb0","ca2":"Ta1","ca3":"Tb1","cb2":"Ta2","ga1":"factors","d1":"ca1","dwa":"ca1"}

        def place(shape, dtype, size, name, room):
            if name in pins:
                base, fill = rooms[pins[name]]
                start = base + fill
                rooms[pins[name]] = (base, fill + size)
            else:
                start = top[0]
                top[0] = top[0] + size
            if room:
                rooms[room] = (start, 0)
            return shared.tile(shape, dtype, name=name, offset=start, align_bytes=64)

        tokens = [place([P, C], F32, 4 * C, "x%d" % k, "gb%d" % k) for k in range(TILES)]
        first_picks = top[0]
        top[0] = top[0] + 8 * K
        factors = shared.tile([P, 16], F32, name="factors", offset=first_picks + 4 * K - 32)
        factor_a, factor_b = factors[:, 0:PACK], factors[:, 8 : 8 + PACK]
        rooms["factors"] = (first_picks, 0)
        wa_raw = keep.tile([P, K], U16, name="wa_raw")
        wb_raw = keep.tile([P, K], U16, name="wb_raw")
        va_raw = keep.tile([P, K], I32, name="va_raw")
        scales_raw = place([P, 2 * K], U8, 4 * K, "scales_raw", "d2")
        first_raw, second_raw = scales_raw[:, 0:K], scales_raw[:, K : 2 * K]
        ident = keep.tile([P, P], F32, name="ident")

        nc.gpsimd.memset(scales_raw[:].bitcast(U32), 0)
        make_identity(nc, ident[:])

        t = {}
        out_scales = keep.tile([P, T], U8, name="out_scales", align_bytes=64)
        out_rows = out_0.rearrange("(p j) t -> p j t", j=PACK)
        out_words = out_1[0].rearrange("p t r -> p (t r)").bitcast(I32)
        queues = {"sp": nc.sync, "act": nc.scalar}
        planes = {"wa": (first_raw, 0, wa_scales), "wb": (second_raw, 0, wb_scales), "va": (second_raw, 4, va_scales)}

        def load(queue, name):
            if name == "o1":
                queue.dma_start(list_a[:], offs)
            elif name == "o2":
                queue.dma_start(list_b[:], offs2)
            elif name == "fi":
                queue.dma_start(out=factor_a[:], in_=fi.rearrange("(p j) o -> p (j o)", j=PACK))
            elif name == "fj":
                queue.dma_start(out=factor_b[:], in_=fj.rearrange("(p j) o -> p (j o)", j=PACK))
            elif name[0] == "x":
                k = int(name[1])
                queue.dma_start(out=tokens[k][:], in_=xt[k * P : (k + 1) * P, :])
            elif name == "wa":
                queue.dma_start(out=wa_raw[:].bitcast(I32), in_=wa_words[0].bitcast(I32))
            elif name == "wb":
                queue.dma_start(out=wb_raw[:].bitcast(I32), in_=wb_words[0].bitcast(I32))
            elif name == "va":
                queue.dma_start(out=va_raw[:], in_=va_words[0].rearrange("p n t -> p (n t)").bitcast(I32))
            else:
                plane, row, scales = planes[name[1:3]]
                q = int(name[3])
                queue.dma_start(
                    out=plane[32 * q + row : 32 * q + row + 4, :].bitcast(I32),
                    in_=scales[0, 4 * q : 4 * q + 4, :].bitcast(I32),
                )

        def step(name):
            kind, key = name[0], name[1:]
            if name[0:2] == "L:":
                parts = name.split(":")
                load(queues[parts[1]], parts[2])
            elif name[0:3] == "row":
                factor = factor_a if name == "rowa" else factor_b
                bank = turn_ps.tile([P, PACK, P], F32, tag="turn", name=name + "_bank")
                for j in range(PACK):
                    nc.tensor.transpose(bank[:, j, :], factor[:, j : j + 1].to_broadcast([P, P]), ident[:])
                t[name] = place([P, K], F32, 8 * K, name, "g" + name[3] + "last")
                dst, src = t[name][:].rearrange("q (n j) -> q n j", j=PACK), bank[:].rearrange("q j n -> q n j")
                nc.vector.tensor_copy(out=dst, in_=src)
            elif kind == "d":
                raw, dtype, size = {"wa": (wa_raw, U16, 2), "wb": (wb_raw, U16, 2), "va": (va_raw, I32, 4), "1": (first_raw, U8, 1), "2": (second_raw, U8, 1)}[key]
                t[name] = place([P, K], dtype, size * K, name, None)
                nc.vector.tensor_copy(
                    out=t[name][:].rearrange("p (j q) -> p j q", j=PACK), in_=raw[:].rearrange("p (q j) -> p j q", j=PACK)
                )
            elif kind == "g":
                t[name] = place([P, K], F32, 4 * K, name, "c" + key)
                offsets = list_a if key[0] == "a" else list_b
                nc.vector.tensor_tensor(t[name][:], tokens[int(key[1])][:].indirect(offsets[:]), t["row" + key[0]][:], MULT)
            elif kind == "c":
                t[name] = place([P, K], BF16, 2 * K, name, "T" + key)
                dst = t[name][:].rearrange("t (u p e) -> t u p e", u=2, e=2)
                src = t["g" + key][:].rearrange("t (p u e) -> t u p e", u=2, e=2)
                if name in ["cb3"]:
                    nc.vector.tensor_copy(out=dst, in_=src)
                else:
                    nc.scalar.activation(out=dst, in_=src, func=COPY)
            elif kind == "T":
                words = t["c" + key][:].bitcast(F32)
                t[name] = turn_ps.tile([P, PACK, P], F32, tag="turn", name=name)
                for u in range(2):
                    nc.tensor.transpose(t[name][:, u, :], words[:, u * P : (u + 1) * P], ident[:])
            elif kind == "e":
                t[name] = place([P, K], BF16, 4 * K, name, "q" + key)
                nc.scalar.copy(
                    out=t[name][:].bitcast(F32).rearrange("p (t u) -> p t u", u=2),
                    in_=t["T" + key][:, 0:2, :].rearrange("p u t -> p t u"),
                )
            elif kind == "q":
                k = int(key[1])
                src = t[{"a": "ea", "b": "eb", "h": "r", "y": "yb"}[key[0]] + key[1]]
                codes = place([P, P], U32, 4 * P, name, None)
                if key[0] == "y":
                    cols = slice(k * P, (k + 1) * P)
                    nc.vector.quantize_mx(out=codes[:].bitcast(FP8X4), scales=out_scales[:, cols], in_=src[:])
                    nc.sync.dma_start(out=out_words[:, cols], in_=codes[:].bitcast(I32))
                else:
                    scales = keep.tile([P, P], U8, name=name + "_scales", align_bytes=64)
                    nc.vector.quantize_mx(out=codes[:].bitcast(FP8X4), scales=scales[:], in_=src[:])
                    t[name] = (codes, scales)
            elif kind == "m":
                k = key[1]
                weight, dtype, plane, row, operand = {
                    "1": ("dwa", FP4X4, "d1", 0, "qa"), "b": ("dwb", FP4X4, "d2", 0, "qb"), "v": ("dva", FP8X4, "d2", 4, "qh"),
                }[key[0]]
                codes, scales = t[operand + k]
                if key[0] == "1":
                    bank = hid_ps.tile([P, PACK, P], F32, tag="hid", name=name)
                    t["hid" + k] = bank
                    first, last = True, True
                elif "out" + k in t:
                    bank = t["out" + k]
                    first, last = False, True
                else:
                    bank = out_ps.tile([P, PACK, P], F32, tag="out", name=name)
                    t["out" + k] = bank
                    first, last = True, False
                for j in range(PACK):
                    cols = slice(j * P, (j + 1) * P)
                    alone = key[0] == "1"
                    nc.tensor.matmul_mx(
                        out=bank[:, j, :], lhsT=t[weight][:, cols].bitcast(dtype), lhsT_scale=t[plane][row:P, cols],
                        rhs=codes[:].bitcast(FP8X4), rhs_scale=scales[:],
                        start=first and (alone or j == 0), stop=last and (alone or j == PACK - 1),
                    )
            elif kind == "r":
                t[name] = place([P, K], BF16, 2 * K, name, "qh" + key)
                nc.scalar.activation(
                    out=t[name][:].rearrange("p (t j) -> p t j", j=PACK), in_=t["hid" + key][:].rearrange("p j t -> p t j"), func=RELU
                )
            elif name[0:2] == "yf":
                k = int(name[2])
                t[name] = place([P, PACK, P], F32, 4 * K, name, None)
                nc.scalar.copy(out=t[name][:], in_=t["out" + name[2]][:])
                nc.sync.dma_start(out=out_rows[:, :, k * P : (k + 1) * P], in_=t[name][:])
            elif name[0:2] == "yb":
                t[name] = place([P, K], BF16, 2 * K, name, "qy" + name[2])
                nc.vector.tensor_copy(
                    out=t[name][:].rearrange("p (t j) -> p t j", j=PACK), in_=t["yf" + name[2]][:].rearrange("p j t -> p t j")
                )

        for name in "L:sp:o1 L:act:fi L:sp:o2 L:act:fj L:sp:x0 L:act:swa0 L:act:swa1 L:act:swa2 L:act:swa3 rowa rowb L:sp:wa L:sp:x1 L:sp:x2 L:sp:wb L:sp:va L:sp:x3 L:sp:swb0 L:sp:swb1 L:sp:swb2 L:sp:swb3 L:sp:sva0 L:sp:sva1 L:sp:sva2 L:sp:sva3 ga0 ca0 Ta0 gb0 cb0 Tb0 ea0 ga1 ca1 Ta1 eb0 gb1 cb1 Tb1 ea1 d1 dwa qa0 m10 qb0 ga2 ca2 Ta2 eb1 r0 qa1 m11 ga3 ca3 Ta3 ea2 r1 qb1 gb2 cb2 Tb2 ea3 qa2 m12 dwb dva qh0 qh1 d2 qa3 m13 mb0 mv0 mb1 mv1 eb2 r2 r3 yf0 yf1 gb3 cb3 Tb3 eb3 qh2 qb2 qh3 qb3 mb2 mv2 mv3 mb3 yf2 yf3 yb0 qy0 yb1 qy1 yb2 qy2 yb3 qy3".split():
            step(name)

        for q in range(4):
            queue = nc.sync if q < 2 else nc.scalar
            queue.dma_start(
                out=out_2[0, 4 * q : 4 * q + 4, :].bitcast(I32), in_=out_scales[32 * q : 32 * q + 4, :].bitcast(I32)
            )
